import numpy as np
import ml_dtypes


def mxq(x, axis, fmt="e4m3"):
    dtype, down = {"e4m3": (ml_dtypes.float8_e4m3fn, 7), "e5m2": (ml_dtypes.float8_e5m2, 14)}[fmt]
    v = np.moveaxis(np.asarray(x, np.float32).astype(ml_dtypes.bfloat16).astype(np.float64), axis, -1)
    blocks = v.reshape(v.shape[:-1] + (-1, 32))
    amax = np.abs(blocks).max(-1, keepdims=True)
    byte = np.maximum(np.where(amax > 0, np.frexp(amax)[1] - 1 + 127, 0) - down, 1)
    scale = np.exp2(byte - 127.0)
    codes = (blocks / scale).astype(np.float32).astype(dtype).astype(np.float64)
    return np.moveaxis((codes * scale).reshape(v.shape), -1, axis)


WIDE = False


def mx_kscale(k):
    if not WIDE:
        return np.ones(k)
    levels = np.array([30, -30])
    if k % 512:
        return np.exp2(np.random.permutation(np.resize(levels, k // 32))).repeat(32)
    a = np.empty((k // 512, 16))
    for p in range(k // 512):
        a[p, :8] = np.random.permutation(np.resize(levels, 8))
        for g in range(8):
            far = levels[np.abs(levels - a[p, g]) >= 10]
            a[p, g + 8] = far[np.random.randint(len(far))]
    return np.exp2(a.ravel()).repeat(32)


def f64(x):
    return np.asarray(x).astype(np.float64)


def striped(idx):
    return np.tile(np.asarray(idx).reshape(-1, 16).T, (8, 1)).astype(np.uint16)


def unstriped(offs):
    return offs[:16].T.reshape(-1).astype(np.int64)


E2M1 = np.array([0.0, 0.5, 1.0, 1.5, 2.0, 3.0, 4.0, 6.0, -0.0, -0.5, -1.0, -1.5, -2.0, -3.0, -4.0, -6.0])


def pack_weight(w, fmt):
    k, n = w.shape
    w = f64(np.asarray(w, np.float32).astype(ml_dtypes.bfloat16)).reshape(k // 32, 32, n)
    amax = np.abs(w).max(1)
    if fmt == "e4m3":
        byte = np.frexp(amax)[1] - 1 + 127 - 7
    else:
        mant, ex = np.frexp(amax / 6.0)
        byte = np.where(mant > 0.5, ex, ex - 1) + 127
    byte = np.clip(np.where(amax > 0, byte, 1), 1, 254)
    scaled = (w * np.exp2(127.0 - byte)[:, None, :]).reshape(k, n).astype(np.float32)
    by_word = np.ascontiguousarray(scaled.reshape(k // 512, 128, 4, n).transpose(0, 1, 3, 2))
    if fmt == "e4m3":
        words = by_word.astype(ml_dtypes.float8_e4m3fn).view(np.uint8)
    else:
        c = by_word.astype(ml_dtypes.float4_e2m1fn).view(np.uint8) & 0xF
        words = (c[..., 0::2] | (c[..., 1::2] << 4)).reshape(k // 512, 128, 2 * n)
    return np.ascontiguousarray(words), np.ascontiguousarray(byte.astype(np.uint8).reshape(k // 512, 16, n))


def unpack_weight(words, scales, fmt):
    g, _, n = scales.shape
    words = np.ascontiguousarray(words).reshape(g, 128, n, -1)
    if fmt == "e4m3":
        vals = words.view(ml_dtypes.float8_e4m3fn).astype(np.float64)
    else:
        nib = np.empty((g, 128, n, 4), np.uint8)
        nib[..., 0::2] = words & 0xF
        nib[..., 1::2] = words >> 4
        vals = E2M1[nib]
    vals = vals * np.repeat(np.exp2(scales.astype(np.float64) - 127.0), 8, axis=1)[..., None]
    return vals.transpose(0, 1, 3, 2).reshape(g * 512, n)


K, J, N, R, T, V = 512, 512, 256, 256, 1024, 1024


def setup_inputs():
    n = np.random.standard_normal
    idx = np.random.permutation(T)[:J]
    idx2 = np.random.permutation(V)[:J]
    fj = mx_kscale(J)
    fk = mx_kscale(K)
    drp = pack_weight(n((K, R)) * 1 / np.sqrt(K) / fk[:, None], "e2m1")
    return {
        "xf": (n((K, T))).astype(np.float32),
        "ra": (np.random.uniform(0.5, 1.5, (1, J)) * fj).astype(np.float32),
        "ow": (n((K, J)) * 0.7).astype(np.float32),
        "gt": (n((N, V)) * np.exp(0.5 * n((1, V)))).astype(np.float32),
        "rb": (np.random.uniform(0.5, 1.5, (1, J)) / fj).astype(np.float32),
        "fkr": (np.random.uniform(0.5, 1.5, (1, K)) * fk).astype(np.float32),
        "dr_words": drp[0],
        "dr_scales": drp[1],
        "bn": (np.random.uniform(-12.0, 12.0, (1, N))).astype(np.float32),
        "offs": striped(idx),
        "offs2": striped(idx2),
    }


def reference(xf, ra, ow, gt, rb, fkr, dr_words, dr_scales, bn, offs, offs2):
    idx = unstriped(offs)
    idx2 = unstriped(offs2)
    dru = unpack_weight(dr_words, dr_scales, "e2m1")
    us = (f64(xf)[:, idx] - f64(ow)) * f64(ra)
    ut = us.T
    uj = ut * f64(fkr)
    gs = f64(gt)[:, idx2] * f64(rb)
    gj = gs.T
    ujq = mxq(uj, 0, "e4m3")
    gjq = mxq(gj, 0, "e5m2")
    w = ujq.T @ gjq
    wq = mxq(w, 0, "e5m2")
    v2 = dru.T @ wq
    wv = v2 + f64(bn)
    mn = np.mean(wv, axis=1, keepdims=True)
    dw = wv - mn
    y = dw / (np.mean(np.abs(dw), axis=1, keepdims=True) + 2.0)
    return y

@@ -1,0 +1,211 @@
+from contextlib import ExitStack
+
+import concourse.mybir as mybir
+from concourse.masks import make_identity
+
+K, J, N, R, T, V = 512, 512, 256, 256, 1024, 1024
+FLOPS = 2 * J * K * N + 2 * K * R * N
+
+F32 = mybir.dt.float32
+BF16 = mybir.dt.bfloat16
+I32 = mybir.dt.int32
+U32 = mybir.dt.uint32
+U16 = mybir.dt.uint16
+U8 = mybir.dt.uint8
+E4M3 = mybir.dt.float8_e4m3fn_x4
+E5M2 = mybir.dt.float8_e5m2_x4
+E2M1 = mybir.dt.float4_e2m1fn_x4
+ALU = mybir.AluOpType
+ACT = mybir.ActivationFunctionType
+
+P = 128
+PACK = 4
+PER_COL = 16
+X_FUSED = 128
+G_FUSED = 256
+
+
+def tile_list_directions_offset_listed_spread_kernel(
+    tc, xf, ra, ow, gt, rb, fkr, dr_words, dr_scales, bn, offs, offs2, out
+):
+    nc = tc.nc
+    with ExitStack() as ctx:
+        keep = ctx.enter_context(tc.tile_pool(name="keep", bufs=1))
+        ps_turn = ctx.enter_context(tc.psum_pool(name="ps_turn", bufs=3))
+        ps_sum = ctx.enter_context(tc.psum_pool(name="ps_sum", bufs=1))
+
+        def tiles(name, count, shape, dtype):
+            return [keep.tile(shape, dtype, name=f"{name}{i}", align_bytes=64) for i in range(count)]
+
+        x_list = keep.tile([P, J // PER_COL], U16, name="x_list")
+        g_list = keep.tile([P, J // PER_COL], U16, name="g_list")
+        x_rows = tiles("x_rows", PACK, [P, T], F32)
+        ow_rows = tiles("ow_rows", PACK, [P, J], F32)
+        g_rows = tiles("g_rows", 2, [P, V], F32)
+        ra_col = keep.tile([P, PACK], F32, name="ra_col")
+        rb_col = keep.tile([P, PACK], F32, name="rb_col")
+        fk_col = keep.tile([P, PACK], F32, name="fk_col")
+        bn_col = keep.tile([P, 2], F32, name="bn_col")
+        dr_codes = keep.tile([P, 2 * R], U8, name="dr_codes", align_bytes=64)
+        dr_plane = keep.tile([P, R], U8, name="dr_plane", align_bytes=64)
+        ident = keep.tile([P, P], F32, name="ident")
+
+        xf_dealt = xf.rearrange("(m s) t -> s m t", s=PACK)
+        ow_dealt = ow.rearrange("(m s) j -> s m j", s=PACK)
+
+        nc.scalar.dma_start(out=ra_col[:], in_=ra.rearrange("o (p t) -> (o p) t", t=PACK))
+        nc.scalar.dma_start(out=fk_col[:], in_=fkr.rearrange("o (p t) -> (o p) t", t=PACK))
+        nc.scalar.dma_start(out=rb_col[:], in_=rb.rearrange("o (p t) -> (o p) t", t=PACK))
+        nc.scalar.dma_start(out=bn_col[:], in_=bn.rearrange("o (p t) -> (o p) t", t=2))
+        nc.sync.dma_start(out=x_list[:], in_=offs)
+        for s in range(2):
+            nc.sync.dma_start(out=x_rows[s][:], in_=xf_dealt[s])
+            nc.sync.dma_start(out=ow_rows[s][:], in_=ow_dealt[s])
+        nc.sync.dma_start(out=g_list[:], in_=offs2)
+        nc.sync.dma_start(out=g_rows[0][:], in_=gt[0:P, :])
+        for s in range(2, PACK):
+            nc.sync.dma_start(out=x_rows[s][:], in_=xf_dealt[s])
+            nc.sync.dma_start(out=ow_rows[s][:], in_=ow_dealt[s])
+        nc.sync.dma_start(out=g_rows[1][:], in_=gt[P : 2 * P, :])
+
+        make_identity(nc, ident[:])
+        nc.gpsimd.memset(dr_plane[:].bitcast(I32), 0)
+        nc.gpsimd.dma_start(out=dr_codes[:].bitcast(I32), in_=dr_words[0].bitcast(I32))
+        for q in range(4):
+            nc.gpsimd.dma_start(
+                out=dr_plane[32 * q : 32 * q + 4, :].bitcast(I32),
+                in_=dr_scales[0, 4 * q : 4 * q + 4, :].bitcast(I32),
+            )
+
+        def spread(name, col, per):
+            bank = ps_turn.tile([P, per, P], F32, tag="turn", name=f"{name}_bank")
+            for t in range(per):
+                nc.tensor.transpose(bank[:, t, :], col[:, t : t + 1].to_broadcast([P, P]), ident[:])
+            row = keep.tile([P, P * per], F32, name=name)
+            nc.vector.tensor_copy(
+                out=row[:].rearrange("q (p t) -> q p t", t=per),
+                in_=bank[:].rearrange("q t p -> q p t"),
+            )
+            return row
+
+        def turn_and_quantise(name, rounded, fmt):
+            words = rounded[:].bitcast(F32)
+            bank = ps_turn.tile([P, 2, P], F32, tag="turn", name=f"{name}_bank")
+            for u in range(2):
+                nc.tensor.transpose(bank[:, u, :], words[:, u::2], ident[:])
+            grouped = keep.tile([P, PACK * P], BF16, name=f"{name}_grouped", align_bytes=64)
+            nc.scalar.copy(
+                out=grouped[:].bitcast(F32).rearrange("p (c u) -> p c u", u=2),
+                in_=bank[:].rearrange("p u c -> p c u"),
+            )
+            return quantise(name, grouped, fmt)
+
+        def quantise(name, grouped, fmt):
+            codes = keep.tile([P, P], U32, name=f"{name}_codes", align_bytes=64)
+            plane = keep.tile([P, P], U8, name=f"{name}_plane", align_bytes=64)
+            nc.vector.quantize_mx(out=codes[:].bitcast(fmt), scales=plane[:], in_=grouped[:])
+            return codes[:].bitcast(fmt), plane[:]
+
+        def features(s):
+            cut = X_FUSED // PER_COL
+            diff = keep.tile([P, J], F32, name=f"diff{s}")
+            picked = keep.tile([P, J - X_FUSED], F32, name=f"picked{s}")
+            nc.scalar.activation(out=picked[:], in_=x_rows[s][:].indirect(x_list[:, cut:]), func=ACT.Copy)
+            nc.vector.tensor_tensor(
+                out=diff[:, :X_FUSED], in0=x_rows[s][:].indirect(x_list[:, :cut]),
+                in1=ow_rows[s][:, :X_FUSED], op=ALU.subtract,
+            )
+            nc.vector.tensor_tensor(
+                out=diff[:, X_FUSED:], in0=picked[:], in1=ow_rows[s][:, X_FUSED:], op=ALU.subtract
+            )
+            rounded = keep.tile([P, J], BF16, name=f"u_rounded{s}")
+            nc.vector.scalar_tensor_tensor(
+                out=rounded[:], in0=diff[:], scalar=fk_col[:, s : s + 1], in1=ra_row[:],
+                op0=ALU.mult, op1=ALU.mult,
+            )
+            return turn_and_quantise(f"u{s}", rounded, E4M3)
+
+        def gradients(h, fused):
+            cut = fused // PER_COL
+            rounded = keep.tile([P, J], BF16, name=f"g_rounded{h}")
+            picked = keep.tile([P, J - fused], F32, name=f"g_picked{h}")
+            nc.scalar.activation(out=picked[:], in_=g_rows[h][:].indirect(g_list[:, cut:]), func=ACT.Copy)
+            if fused:
+                weighted = keep.tile([P, fused], F32, name=f"g_weighted{h}")
+                nc.vector.tensor_tensor(
+                    out=weighted[:], in0=g_rows[h][:].indirect(g_list[:, :cut]),
+                    in1=rb_row[:, :fused], op=ALU.mult,
+                )
+                nc.scalar.copy(out=rounded[:, :fused], in_=weighted[:])
+            nc.vector.tensor_tensor(out=rounded[:, fused:], in0=picked[:], in1=rb_row[:, fused:], op=ALU.mult)
+            return turn_and_quantise(f"g{h}", rounded, E5M2)
+
+        ra_row = spread("ra_row", ra_col, PACK)
+        rb_row = spread("rb_row", rb_col, PACK)
+        bn_row = spread("bn_row", bn_col, 2)
+        u_mx = [features(0)]
+        u_mx.append(features(1))
+        g_mx = [gradients(0, 0)]
+        u_mx.append(features(2))
+        u_mx.append(features(3))
+        g_mx.append(gradients(1, G_FUSED))
+
+        wv = keep.tile([P, 2, N], F32, name="wv")
+        sums = keep.tile([P, 2, 2], F32, name="sums")
+        for h in range(2):
+            moment = ps_sum.tile([P, PACK, P], F32, name=f"moment{h}")
+            for s in range(PACK):
+                nc.tensor.matmul_mx(
+                    out=moment[:, s, :], lhsT=u_mx[s][0], lhsT_scale=u_mx[s][1],
+                    rhs=g_mx[h][0], rhs_scale=g_mx[h][1], start=True, stop=True,
+                )
+            w_grouped = keep.tile([P, PACK * P], BF16, name=f"w_grouped{h}", align_bytes=64)
+            nc.scalar.copy(
+                out=w_grouped[:].rearrange("p (c s) -> p c s", s=PACK),
+                in_=moment[:].rearrange("p s c -> p c s"),
+            )
+            w_codes, w_plane = quantise(f"w{h}", w_grouped, E5M2)
+            seen = ps_sum.tile([P, 2, P], F32, name=f"seen{h}")
+            for r in range(2):
+                nc.tensor.matmul_mx(
+                    out=seen[:, r, :],
+                    lhsT=dr_codes[:, 2 * P * r : 2 * P * (r + 1)].bitcast(E2M1),
+                    lhsT_scale=dr_plane[:, P * r : P * (r + 1)],
+                    rhs=w_codes, rhs_scale=w_plane, start=True, stop=True,
+                )
+            for r in range(2):
+                nc.vector.scalar_tensor_tensor(
+                    out=wv[:, r, P * h : P * (h + 1)], in0=seen[:, r, :], scalar=1.0,
+                    in1=bn_row[:, P * h : P * (h + 1)], op0=ALU.mult, op1=ALU.add,
+                    accum_out=sums[:, h, r : r + 1],
+                )
+            if h == 0:
+                part_mean = keep.tile([P, 2], F32, name="part_mean")
+                nc.vector.tensor_scalar(
+                    out=part_mean[:], in0=sums[:, 0, :], scalar1=-1.0 / N, scalar2=None, op0=ALU.mult
+                )
+
+        neg_mean = keep.tile([P, 2], F32, name="neg_mean")
+        nc.vector.scalar_tensor_tensor(
+            out=neg_mean[:], in0=sums[:, 1, :], scalar=-1.0 / N, in1=part_mean[:], op0=ALU.mult, op1=ALU.add
+        )
+        magnitude = keep.tile([P, 2, N], F32, name="magnitude")
+        spreads = keep.tile([P, 2], F32, name="spreads")
+        for r in range(2):
+            nc.scalar.activation(
+                out=magnitude[:, r, :], in_=wv[:, r, :], func=ACT.Abs,
+                bias=neg_mean[:, r : r + 1], accum_out=spreads[:, r : r + 1],
+            )
+        divisor = keep.tile([P, 2], F32, name="divisor")
+        nc.vector.tensor_scalar(
+            out=divisor[:], in0=spreads[:], scalar1=1.0 / N, scalar2=2.0, op0=ALU.mult, op1=ALU.add
+        )
+        inverse = keep.tile([P, 2], F32, name="inverse")
+        nc.vector.reciprocal(out=inverse[:], in_=divisor[:])
+        result = tiles("result", 2, [P, N], F32)
+        for r in range(2):
+            nc.vector.tensor_scalar(
+                out=result[r][:], in0=wv[:, r, :], scalar1=neg_mean[:, r : r + 1],
+                scalar2=inverse[:, r : r + 1], op0=ALU.add, op1=ALU.mult,
+            )
+            nc.sync.dma_start(out=out[P * r : P * (r + 1), :], in_=result[r][:])

@@ -1,7 +1,6 @@
 from contextlib import ExitStack
 
 import concourse.mybir as mybir
-from concourse.masks import make_identity
 
 K, J, N, R, T, V = 512, 512, 256, 256, 1024, 1024
 FLOPS = 2 * J * K * N + 2 * K * R * N
@@ -21,8 +20,8 @@ ACT = mybir.ActivationFunctionType
 P = 128
 PACK = 4
 PER_COL = 16
-X_FUSED = 128
-G_FUSED = 256
+X_FUSED = (128, 128, 128, 128)
+G_FUSED = (0, 128)
 
 
 def tile_list_directions_offset_listed_spread_kernel(
@@ -31,11 +30,11 @@ def tile_list_directions_offset_listed_spread_kernel(
     nc = tc.nc
     with ExitStack() as ctx:
         keep = ctx.enter_context(tc.tile_pool(name="keep", bufs=1))
-        ps_turn = ctx.enter_context(tc.psum_pool(name="ps_turn", bufs=3))
+        ps_turn = ctx.enter_context(tc.psum_pool(name="ps_turn", bufs=4))
         ps_sum = ctx.enter_context(tc.psum_pool(name="ps_sum", bufs=1))
 
         def tiles(name, count, shape, dtype):
-            return [keep.tile(shape, dtype, name=f"{name}{i}", align_bytes=64) for i in range(count)]
+            return [keep.tile(shape, dtype, name=f"{name}{i}", tag=f"{name}{i}", align_bytes=64) for i in range(count)]
 
         x_list = keep.tile([P, J // PER_COL], U16, name="x_list")
         g_list = keep.tile([P, J // PER_COL], U16, name="g_list")
@@ -53,47 +52,61 @@ def tile_list_directions_offset_listed_spread_kernel(
         xf_dealt = xf.rearrange("(m s) t -> s m t", s=PACK)
         ow_dealt = ow.rearrange("(m s) j -> s m j", s=PACK)
 
+        nc.scalar.dma_start(out=rb_col[:], in_=rb.rearrange("o (p t) -> (o p) t", t=PACK))
         nc.scalar.dma_start(out=ra_col[:], in_=ra.rearrange("o (p t) -> (o p) t", t=PACK))
         nc.scalar.dma_start(out=fk_col[:], in_=fkr.rearrange("o (p t) -> (o p) t", t=PACK))
-        nc.scalar.dma_start(out=rb_col[:], in_=rb.rearrange("o (p t) -> (o p) t", t=PACK))
         nc.scalar.dma_start(out=bn_col[:], in_=bn.rearrange("o (p t) -> (o p) t", t=2))
-        nc.sync.dma_start(out=x_list[:], in_=offs)
-        for s in range(2):
-            nc.sync.dma_start(out=x_rows[s][:], in_=xf_dealt[s])
-            nc.sync.dma_start(out=ow_rows[s][:], in_=ow_dealt[s])
-        nc.sync.dma_start(out=g_list[:], in_=offs2)
         nc.sync.dma_start(out=g_rows[0][:], in_=gt[0:P, :])
-        for s in range(2, PACK):
+        nc.sync.dma_start(out=g_list[:], in_=offs2)
+        nc.sync.dma_start(out=x_list[:], in_=offs)
+        for s in range(PACK):
             nc.sync.dma_start(out=x_rows[s][:], in_=xf_dealt[s])
             nc.sync.dma_start(out=ow_rows[s][:], in_=ow_dealt[s])
         nc.sync.dma_start(out=g_rows[1][:], in_=gt[P : 2 * P, :])
 
-        make_identity(nc, ident[:])
         nc.gpsimd.memset(dr_plane[:].bitcast(I32), 0)
-        nc.gpsimd.dma_start(out=dr_codes[:].bitcast(I32), in_=dr_words[0].bitcast(I32))
+        nc.sync.dma_start(out=dr_codes[:].bitcast(I32), in_=dr_words[0].bitcast(I32))
         for q in range(4):
-            nc.gpsimd.dma_start(
+            nc.sync.dma_start(
                 out=dr_plane[32 * q : 32 * q + 4, :].bitcast(I32),
                 in_=dr_scales[0, 4 * q : 4 * q + 4, :].bitcast(I32),
             )
 
-        def spread(name, col, per):
+        ones = keep.tile([P, P], F32, name="ones")
+        quadrant = keep.tile([P, 1], F32, name="quadrant")
+        count = keep.tile([P, P], F32, name="count", align_bytes=64)
+        own = keep.tile([P, 32], F32, name="own", align_bytes=64)
+        nc.vector.memset(ones[:], 1.0)
+        for q in range(4):
+            nc.gpsimd.memset(quadrant[32 * q : 32 * (q + 1), :], 32.0 * q)
+        nc.vector.tensor_tensor_scan(
+            out=count[:], data0=ones[:], data1=ones[:], initial=quadrant[:], op0=ALU.mult, op1=ALU.add
+        )
+        nc.vector.transpose(out=own[:], in_=count[:, :32])
+        nc.vector.tensor_scalar(
+            out=ident[:], in0=count[:], scalar1=quadrant[:], scalar2=own[:, 0:1],
+            op0=ALU.subtract, op1=ALU.is_equal,
+        )
+        zero = keep.tile([P, 1], F32, name="zero")
+        nc.scalar.activation(out=zero[:], in_=ones[:, 0:1], func=ACT.Relu, scale=-1.0)
+
+        def spread(name, col, per, copy):
             bank = ps_turn.tile([P, per, P], F32, tag="turn", name=f"{name}_bank")
             for t in range(per):
                 nc.tensor.transpose(bank[:, t, :], col[:, t : t + 1].to_broadcast([P, P]), ident[:])
             row = keep.tile([P, P * per], F32, name=name)
-            nc.vector.tensor_copy(
-                out=row[:].rearrange("q (p t) -> q p t", t=per),
-                in_=bank[:].rearrange("q t p -> q p t"),
-            )
+            copy(out=row[:].rearrange("q (p t) -> q p t", t=per), in_=bank[:].rearrange("q t p -> q p t"))
             return row
 
-        def turn_and_quantise(name, rounded, fmt):
+        def turn(name, rounded):
             words = rounded[:].bitcast(F32)
             bank = ps_turn.tile([P, 2, P], F32, tag="turn", name=f"{name}_bank")
             for u in range(2):
                 nc.tensor.transpose(bank[:, u, :], words[:, u::2], ident[:])
-            grouped = keep.tile([P, PACK * P], BF16, name=f"{name}_grouped", align_bytes=64)
+            return bank
+
+        def group_and_quantise(name, bank, fmt, tag):
+            grouped = keep.tile([P, PACK * P], BF16, name=f"{name}_grouped", tag=tag, align_bytes=64)
             nc.scalar.copy(
                 out=grouped[:].bitcast(F32).rearrange("p (c u) -> p c u", u=2),
                 in_=bank[:].rearrange("p u c -> p c u"),
@@ -107,25 +120,28 @@ def tile_list_directions_offset_listed_spread_kernel(
             return codes[:].bitcast(fmt), plane[:]
 
         def features(s):
-            cut = X_FUSED // PER_COL
+            fused = X_FUSED[s]
+            cut = fused // PER_COL
             diff = keep.tile([P, J], F32, name=f"diff{s}")
-            picked = keep.tile([P, J - X_FUSED], F32, name=f"picked{s}")
+            picked = keep.tile([P, J - fused], F32, name=f"picked{s}")
             nc.scalar.activation(out=picked[:], in_=x_rows[s][:].indirect(x_list[:, cut:]), func=ACT.Copy)
+            if fused:
+                nc.vector.tensor_tensor(
+                    out=diff[:, :fused], in0=x_rows[s][:].indirect(x_list[:, :cut]),
+                    in1=ow_rows[s][:, :fused], op=ALU.subtract,
+                )
             nc.vector.tensor_tensor(
-                out=diff[:, :X_FUSED], in0=x_rows[s][:].indirect(x_list[:, :cut]),
-                in1=ow_rows[s][:, :X_FUSED], op=ALU.subtract,
-            )
-            nc.vector.tensor_tensor(
-                out=diff[:, X_FUSED:], in0=picked[:], in1=ow_rows[s][:, X_FUSED:], op=ALU.subtract
+                out=diff[:, fused:], in0=picked[:], in1=ow_rows[s][:, fused:], op=ALU.subtract
             )
             rounded = keep.tile([P, J], BF16, name=f"u_rounded{s}")
             nc.vector.scalar_tensor_tensor(
                 out=rounded[:], in0=diff[:], scalar=fk_col[:, s : s + 1], in1=ra_row[:],
                 op0=ALU.mult, op1=ALU.mult,
             )
-            return turn_and_quantise(f"u{s}", rounded, E4M3)
+            return turn(f"u{s}", rounded)
 
-        def gradients(h, fused):
+        def gradients(h):
+            fused = G_FUSED[h]
             cut = fused // PER_COL
             rounded = keep.tile([P, J], BF16, name=f"g_rounded{h}")
             picked = keep.tile([P, J - fused], F32, name=f"g_picked{h}")
@@ -138,44 +154,51 @@ def tile_list_directions_offset_listed_spread_kernel(
                 )
                 nc.scalar.copy(out=rounded[:, :fused], in_=weighted[:])
             nc.vector.tensor_tensor(out=rounded[:, fused:], in0=picked[:], in1=rb_row[:, fused:], op=ALU.mult)
-            return turn_and_quantise(f"g{h}", rounded, E5M2)
+            return turn(f"g{h}", rounded)
 
-        ra_row = spread("ra_row", ra_col, PACK)
-        rb_row = spread("rb_row", rb_col, PACK)
-        bn_row = spread("bn_row", bn_col, 2)
-        u_mx = [features(0)]
-        u_mx.append(features(1))
-        g_mx = [gradients(0, 0)]
-        u_mx.append(features(2))
-        u_mx.append(features(3))
-        g_mx.append(gradients(1, G_FUSED))
+        rb_row = spread("rb_row", rb_col, PACK, nc.vector.tensor_copy)
+        ra_row = spread("ra_row", ra_col, PACK, nc.vector.tensor_copy)
+        bn_row = spread("bn_row", bn_col, 2, nc.scalar.copy)
+        g_bank = [gradients(0)]
+        u_bank = [features(0), features(1)]
+        g_mx = [group_and_quantise("g0", g_bank[0], E5M2, "x_rows1")]
+        u_bank.append(features(2))
+        u_mx = [group_and_quantise("u0", u_bank[0], E4M3, "x_rows2")]
+        u_bank.append(features(3))
+        u_mx.append(group_and_quantise("u1", u_bank[1], E4M3, "x_rows3"))
+        g_bank.append(gradients(1))
+        u_mx.append(group_and_quantise("u2", u_bank[2], E4M3, "g_rows1"))
+        u_mx.append(group_and_quantise("u3", u_bank[3], E4M3, "x_rows0"))
+        g_mx.append(group_and_quantise("g1", g_bank[1], E5M2, "g_rows0"))
 
         wv = keep.tile([P, 2, N], F32, name="wv")
         sums = keep.tile([P, 2, 2], F32, name="sums")
+        moment = [ps_sum.tile([P, PACK, P], F32, name=f"moment{h}") for h in range(2)]
+        seen = [ps_sum.tile([P, 2, P], F32, name=f"seen{h}") for h in range(2)]
         for h in range(2):
-            moment = ps_sum.tile([P, PACK, P], F32, name=f"moment{h}")
             for s in range(PACK):
                 nc.tensor.matmul_mx(
-                    out=moment[:, s, :], lhsT=u_mx[s][0], lhsT_scale=u_mx[s][1],
+                    out=moment[h][:, s, :], lhsT=u_mx[s][0], lhsT_scale=u_mx[s][1],
                     rhs=g_mx[h][0], rhs_scale=g_mx[h][1], start=True, stop=True,
                 )
+        for h, copy in enumerate((nc.vector.tensor_copy, nc.scalar.copy)):
             w_grouped = keep.tile([P, PACK * P], BF16, name=f"w_grouped{h}", align_bytes=64)
-            nc.scalar.copy(
+            copy(
                 out=w_grouped[:].rearrange("p (c s) -> p c s", s=PACK),
-                in_=moment[:].rearrange("p s c -> p c s"),
+                in_=moment[h][:].rearrange("p s c -> p c s"),
             )
             w_codes, w_plane = quantise(f"w{h}", w_grouped, E5M2)
-            seen = ps_sum.tile([P, 2, P], F32, name=f"seen{h}")
             for r in range(2):
                 nc.tensor.matmul_mx(
-                    out=seen[:, r, :],
+                    out=seen[h][:, r, :],
                     lhsT=dr_codes[:, 2 * P * r : 2 * P * (r + 1)].bitcast(E2M1),
                     lhsT_scale=dr_plane[:, P * r : P * (r + 1)],
                     rhs=w_codes, rhs_scale=w_plane, start=True, stop=True,
                 )
+        for h in range(2):
             for r in range(2):
                 nc.vector.scalar_tensor_tensor(
-                    out=wv[:, r, P * h : P * (h + 1)], in0=seen[:, r, :], scalar=1.0,
+                    out=wv[:, r, P * h : P * (h + 1)], in0=seen[h][:, r, :], scalar=1.0,
                     in1=bn_row[:, P * h : P * (h + 1)], op0=ALU.mult, op1=ALU.add,
                     accum_out=sums[:, h, r : r + 1],
                 )
@@ -189,16 +212,18 @@ def tile_list_directions_offset_listed_spread_kernel(
         nc.vector.scalar_tensor_tensor(
             out=neg_mean[:], in0=sums[:, 1, :], scalar=-1.0 / N, in1=part_mean[:], op0=ALU.mult, op1=ALU.add
         )
-        magnitude = keep.tile([P, 2, N], F32, name="magnitude")
+        above = tiles("above", 2, [P, N], F32)
         spreads = keep.tile([P, 2], F32, name="spreads")
-        for r in range(2):
-            nc.scalar.activation(
-                out=magnitude[:, r, :], in_=wv[:, r, :], func=ACT.Abs,
-                bias=neg_mean[:, r : r + 1], accum_out=spreads[:, r : r + 1],
-            )
+        nc.scalar.activation(
+            out=above[0][:], in_=wv[:, 0, :], func=ACT.Relu, bias=neg_mean[:, 0:1], accum_out=spreads[:, 0:1]
+        )
+        nc.vector.scalar_tensor_tensor(
+            out=above[1][:], in0=wv[:, 1, :], scalar=neg_mean[:, 1:2], in1=zero[:].to_broadcast([P, N]),
+            op0=ALU.add, op1=ALU.max, accum_out=spreads[:, 1:2],
+        )
         divisor = keep.tile([P, 2], F32, name="divisor")
         nc.vector.tensor_scalar(
-            out=divisor[:], in0=spreads[:], scalar1=1.0 / N, scalar2=2.0, op0=ALU.mult, op1=ALU.add
+            out=divisor[:], in0=spreads[:], scalar1=2.0 / N, scalar2=2.0, op0=ALU.mult, op1=ALU.add
         )
         inverse = keep.tile([P, 2], F32, name="inverse")
         nc.vector.reciprocal(out=inverse[:], in_=divisor[:])

@@ -21,7 +21,7 @@ P = 128
 PACK = 4
 PER_COL = 16
 X_FUSED = (128, 128, 128, 128)
-G_FUSED = (0, 128)
+G_FUSED = (0, 256)
 
 
 def tile_list_directions_offset_listed_spread_kernel(
@@ -87,8 +87,8 @@ def tile_list_directions_offset_listed_spread_kernel(
             out=ident[:], in0=count[:], scalar1=quadrant[:], scalar2=own[:, 0:1],
             op0=ALU.subtract, op1=ALU.is_equal,
         )
-        zero = keep.tile([P, 1], F32, name="zero")
-        nc.scalar.activation(out=zero[:], in_=ones[:, 0:1], func=ACT.Relu, scale=-1.0)
+        unread = keep.tile([P, 1], F32, name="unread")
+        nc.scalar.activation(out=unread[:], in_=ones[:, 0:1], func=ACT.Abs_reciprocal_sqrt)
 
         def spread(name, col, per, copy):
             bank = ps_turn.tile([P, per, P], F32, tag="turn", name=f"{name}_bank")
@@ -171,10 +171,8 @@ def tile_list_directions_offset_listed_spread_kernel(
         u_mx.append(group_and_quantise("u3", u_bank[3], E4M3, "x_rows0"))
         g_mx.append(group_and_quantise("g1", g_bank[1], E5M2, "g_rows0"))
 
-        wv = keep.tile([P, 2, N], F32, name="wv")
-        sums = keep.tile([P, 2, 2], F32, name="sums")
         moment = [ps_sum.tile([P, PACK, P], F32, name=f"moment{h}") for h in range(2)]
-        seen = [ps_sum.tile([P, 2, P], F32, name=f"seen{h}") for h in range(2)]
+        seen = [ps_sum.tile([P, N], F32, name=f"seen{r}") for r in range(2)]
         for h in range(2):
             for s in range(PACK):
                 nc.tensor.matmul_mx(
@@ -190,47 +188,45 @@ def tile_list_directions_offset_listed_spread_kernel(
             w_codes, w_plane = quantise(f"w{h}", w_grouped, E5M2)
             for r in range(2):
                 nc.tensor.matmul_mx(
-                    out=seen[h][:, r, :],
+                    out=seen[r][:, P * h : P * (h + 1)],
                     lhsT=dr_codes[:, 2 * P * r : 2 * P * (r + 1)].bitcast(E2M1),
                     lhsT_scale=dr_plane[:, P * r : P * (r + 1)],
                     rhs=w_codes, rhs_scale=w_plane, start=True, stop=True,
                 )
-        for h in range(2):
-            for r in range(2):
-                nc.vector.scalar_tensor_tensor(
-                    out=wv[:, r, P * h : P * (h + 1)], in0=seen[h][:, r, :], scalar=1.0,
-                    in1=bn_row[:, P * h : P * (h + 1)], op0=ALU.mult, op1=ALU.add,
-                    accum_out=sums[:, h, r : r + 1],
-                )
-            if h == 0:
-                part_mean = keep.tile([P, 2], F32, name="part_mean")
-                nc.vector.tensor_scalar(
-                    out=part_mean[:], in0=sums[:, 0, :], scalar1=-1.0 / N, scalar2=None, op0=ALU.mult
-                )
 
-        neg_mean = keep.tile([P, 2], F32, name="neg_mean")
-        nc.vector.scalar_tensor_tensor(
-            out=neg_mean[:], in0=sums[:, 1, :], scalar=-1.0 / N, in1=part_mean[:], op0=ALU.mult, op1=ALU.add
-        )
-        above = tiles("above", 2, [P, N], F32)
-        spreads = keep.tile([P, 2], F32, name="spreads")
-        nc.scalar.activation(
-            out=above[0][:], in_=wv[:, 0, :], func=ACT.Relu, bias=neg_mean[:, 0:1], accum_out=spreads[:, 0:1]
-        )
-        nc.vector.scalar_tensor_tensor(
-            out=above[1][:], in0=wv[:, 1, :], scalar=neg_mean[:, 1:2], in1=zero[:].to_broadcast([P, N]),
-            op0=ALU.add, op1=ALU.max, accum_out=spreads[:, 1:2],
-        )
-        divisor = keep.tile([P, 2], F32, name="divisor")
-        nc.vector.tensor_scalar(
-            out=divisor[:], in0=spreads[:], scalar1=2.0 / N, scalar2=2.0, op0=ALU.mult, op1=ALU.add
-        )
-        inverse = keep.tile([P, 2], F32, name="inverse")
-        nc.vector.reciprocal(out=inverse[:], in_=divisor[:])
+        wv = tiles("wv", 2, [P, N], F32)
+        total = tiles("total", 2, [P, 1], F32)
+        below = tiles("below", 2, [P, N], F32)
+        below_sum = tiles("below_sum", 2, [P, 1], F32)
+        mean = tiles("mean", 2, [P, 1], F32)
+        centred = tiles("centred", 2, [P, N], F32)
+        root = tiles("root", 2, [P, 1], F32)
         result = tiles("result", 2, [P, N], F32)
         for r in range(2):
+            nc.vector.scalar_tensor_tensor(
+                out=wv[r][:], in0=seen[r][:], scalar=1.0, in1=bn_row[:], op0=ALU.mult, op1=ALU.add,
+                accum_out=total[r][:],
+            )
+        for r in range(2):
+            nc.scalar.activation(
+                out=below[r][:], in_=wv[r][:], func=ACT.Relu, scale=-float(N), bias=total[r][:],
+                accum_out=below_sum[r][:],
+            )
+        for r in range(2):
             nc.vector.tensor_scalar(
-                out=result[r][:], in0=wv[:, r, :], scalar1=neg_mean[:, r : r + 1],
-                scalar2=inverse[:, r : r + 1], op0=ALU.add, op1=ALU.mult,
+                out=mean[r][:], in0=total[r][:], scalar1=1.0 / N, scalar2=None, op0=ALU.mult
+            )
+        for r in range(2):
+            nc.vector.tensor_scalar(
+                out=centred[r][:], in0=wv[r][:], scalar1=mean[r][:], scalar2=None, op0=ALU.subtract
+            )
+        for r in range(2):
+            nc.scalar.activation(
+                out=root[r][:], in_=below_sum[r][:], func=ACT.Abs_reciprocal_sqrt, scale=2.0 / (N * N), bias=2.0
+            )
+        for r in range(2):
+            nc.vector.tensor_scalar(
+                out=result[r][:], in0=centred[r][:], scalar1=root[r][:], scalar2=root[r][:],
+                op0=ALU.mult, op1=ALU.mult,
             )
             nc.sync.dma_start(out=out[P * r : P * (r + 1), :], in_=result[r][:])

@@ -20,8 +20,8 @@ ACT = mybir.ActivationFunctionType
 P = 128
 PACK = 4
 PER_COL = 16
-X_FUSED = (128, 128, 128, 128)
-G_FUSED = (0, 256)
+X_FUSED = (0, 0, 0, 0)
+G_FUSED = (0, 128)
 
 
 def tile_list_directions_offset_listed_spread_kernel(
@@ -54,15 +54,17 @@ def tile_list_directions_offset_listed_spread_kernel(
 
         nc.scalar.dma_start(out=rb_col[:], in_=rb.rearrange("o (p t) -> (o p) t", t=PACK))
         nc.scalar.dma_start(out=ra_col[:], in_=ra.rearrange("o (p t) -> (o p) t", t=PACK))
-        nc.scalar.dma_start(out=fk_col[:], in_=fkr.rearrange("o (p t) -> (o p) t", t=PACK))
-        nc.scalar.dma_start(out=bn_col[:], in_=bn.rearrange("o (p t) -> (o p) t", t=2))
         nc.sync.dma_start(out=g_rows[0][:], in_=gt[0:P, :])
         nc.sync.dma_start(out=g_list[:], in_=offs2)
         nc.sync.dma_start(out=x_list[:], in_=offs)
         for s in range(PACK):
             nc.sync.dma_start(out=x_rows[s][:], in_=xf_dealt[s])
+            if s == 1:
+                nc.sync.dma_start(out=fk_col[:], in_=fkr.rearrange("o (p t) -> (o p) t", t=PACK))
+            if s == PACK - 1:
+                nc.sync.dma_start(out=g_rows[1][:], in_=gt[P : 2 * P, :])
             nc.sync.dma_start(out=ow_rows[s][:], in_=ow_dealt[s])
-        nc.sync.dma_start(out=g_rows[1][:], in_=gt[P : 2 * P, :])
+        nc.sync.dma_start(out=bn_col[:], in_=bn.rearrange("o (p t) -> (o p) t", t=2))
 
         nc.gpsimd.memset(dr_plane[:].bitcast(I32), 0)
         nc.sync.dma_start(out=dr_codes[:].bitcast(I32), in_=dr_words[0].bitcast(I32))
@@ -90,11 +92,10 @@ def tile_list_directions_offset_listed_spread_kernel(
         unread = keep.tile([P, 1], F32, name="unread")
         nc.scalar.activation(out=unread[:], in_=ones[:, 0:1], func=ACT.Abs_reciprocal_sqrt)
 
-        def spread(name, col, per, copy):
-            bank = ps_turn.tile([P, per, P], F32, tag="turn", name=f"{name}_bank")
+        def spread(name, col, per, bank, copy, tag):
             for t in range(per):
                 nc.tensor.transpose(bank[:, t, :], col[:, t : t + 1].to_broadcast([P, P]), ident[:])
-            row = keep.tile([P, P * per], F32, name=name)
+            row = keep.tile([P, P * per], F32, name=name, tag=tag)
             copy(out=row[:].rearrange("q (p t) -> q p t", t=per), in_=bank[:].rearrange("q t p -> q p t"))
             return row
 
@@ -105,19 +106,20 @@ def tile_list_directions_offset_listed_spread_kernel(
                 nc.tensor.transpose(bank[:, u, :], words[:, u::2], ident[:])
             return bank
 
-        def group_and_quantise(name, bank, fmt, tag):
-            grouped = keep.tile([P, PACK * P], BF16, name=f"{name}_grouped", tag=tag, align_bytes=64)
-            nc.scalar.copy(
-                out=grouped[:].bitcast(F32).rearrange("p (c u) -> p c u", u=2),
-                in_=bank[:].rearrange("p u c -> p c u"),
-            )
-            return quantise(name, grouped, fmt)
+        def group_and_quantise(name, banks, fmt, tag):
+            grouped = keep.tile([P, len(banks) * J], BF16, name=f"{name}_grouped", tag=tag, align_bytes=64)
+            for i, bank in enumerate(banks):
+                nc.scalar.copy(
+                    out=grouped[:, J * i : J * (i + 1)].bitcast(F32).rearrange("p (c u) -> p c u", u=2),
+                    in_=bank[:].rearrange("p u c -> p c u"),
+                )
+            return quantise(name, grouped, fmt, len(banks))
 
-        def quantise(name, grouped, fmt):
-            codes = keep.tile([P, P], U32, name=f"{name}_codes", align_bytes=64)
-            plane = keep.tile([P, P], U8, name=f"{name}_plane", align_bytes=64)
+        def quantise(name, grouped, fmt, count):
+            codes = keep.tile([P, count * P], U32, name=f"{name}_codes", align_bytes=64)
+            plane = keep.tile([P, count * P], U8, name=f"{name}_plane", align_bytes=64)
             nc.vector.quantize_mx(out=codes[:].bitcast(fmt), scales=plane[:], in_=grouped[:])
-            return codes[:].bitcast(fmt), plane[:]
+            return [(codes[:, P * i : P * (i + 1)].bitcast(fmt), plane[:, P * i : P * (i + 1)]) for i in range(count)]
 
         def features(s):
             fused = X_FUSED[s]
@@ -143,7 +145,7 @@ def tile_list_directions_offset_listed_spread_kernel(
         def gradients(h):
             fused = G_FUSED[h]
             cut = fused // PER_COL
-            rounded = keep.tile([P, J], BF16, name=f"g_rounded{h}")
+            rounded = keep.tile([P, J], BF16, name=f"g_rounded{h}", tag=f"g_rounded{h}")
             picked = keep.tile([P, J - fused], F32, name=f"g_picked{h}")
             nc.scalar.activation(out=picked[:], in_=g_rows[h][:].indirect(g_list[:, cut:]), func=ACT.Copy)
             if fused:
@@ -156,23 +158,27 @@ def tile_list_directions_offset_listed_spread_kernel(
             nc.vector.tensor_tensor(out=rounded[:, fused:], in0=picked[:], in1=rb_row[:, fused:], op=ALU.mult)
             return turn(f"g{h}", rounded)
 
-        rb_row = spread("rb_row", rb_col, PACK, nc.vector.tensor_copy)
-        ra_row = spread("ra_row", ra_col, PACK, nc.vector.tensor_copy)
-        bn_row = spread("bn_row", bn_col, 2, nc.scalar.copy)
+        def weights_row(name, col):
+            bank = ps_turn.tile([P, PACK, P], F32, tag="turn", name=f"{name}_bank")
+            return spread(name, col, PACK, bank, nc.vector.tensor_copy, name)
+
+        rb_row = weights_row("rb_row", rb_col)
+        ra_row = weights_row("ra_row", ra_col)
         g_bank = [gradients(0)]
         u_bank = [features(0), features(1)]
-        g_mx = [group_and_quantise("g0", g_bank[0], E5M2, "x_rows1")]
+        g_mx = group_and_quantise("g0", g_bank[:1], E5M2, "x_rows1")
         u_bank.append(features(2))
-        u_mx = [group_and_quantise("u0", u_bank[0], E4M3, "x_rows2")]
+        u_mx = group_and_quantise("u0", u_bank[:1], E4M3, "x_rows2")
         u_bank.append(features(3))
-        u_mx.append(group_and_quantise("u1", u_bank[1], E4M3, "x_rows3"))
         g_bank.append(gradients(1))
-        u_mx.append(group_and_quantise("u2", u_bank[2], E4M3, "g_rows1"))
-        u_mx.append(group_and_quantise("u3", u_bank[3], E4M3, "x_rows0"))
-        g_mx.append(group_and_quantise("g1", g_bank[1], E5M2, "g_rows0"))
+        u_mx.extend(group_and_quantise("u12", u_bank[1:3], E4M3, "g_rows1"))
+        g_mx.extend(group_and_quantise("g1", g_bank[1:], E5M2, "g_rows0"))
+        u_mx.extend(group_and_quantise("u3", u_bank[3:], E4M3, "x_rows0"))
+        bn_bank = ps_sum.tile([P, 2, P], F32, tag="seen1", name="bn_bank")
+        bn_row = spread("bn_row", bn_col, 2, bn_bank, nc.scalar.copy, "g_rounded1")
 
         moment = [ps_sum.tile([P, PACK, P], F32, name=f"moment{h}") for h in range(2)]
-        seen = [ps_sum.tile([P, N], F32, name=f"seen{r}") for r in range(2)]
+        seen = [ps_sum.tile([P, N], F32, name=f"seen{r}", tag=f"seen{r}") for r in range(2)]
         for h in range(2):
             for s in range(PACK):
                 nc.tensor.matmul_mx(
@@ -185,7 +191,7 @@ def tile_list_directions_offset_listed_spread_kernel(
                 out=w_grouped[:].rearrange("p (c s) -> p c s", s=PACK),
                 in_=moment[h][:].rearrange("p s c -> p c s"),
             )
-            w_codes, w_plane = quantise(f"w{h}", w_grouped, E5M2)
+            w_codes, w_plane = quantise(f"w{h}", w_grouped, E5M2, 1)[0]
             for r in range(2):
                 nc.tensor.matmul_mx(
                     out=seen[r][:, P * h : P * (h + 1)],

from contextlib import ExitStack

import concourse.mybir as mybir

K, J, N, R, T, V = 512, 512, 256, 256, 1024, 1024
FLOPS = 2 * J * K * N + 2 * K * R * N

F32 = mybir.dt.float32
BF16 = mybir.dt.bfloat16
I32 = mybir.dt.int32
U32 = mybir.dt.uint32
U16 = mybir.dt.uint16
U8 = mybir.dt.uint8
E4M3 = mybir.dt.float8_e4m3fn_x4
E5M2 = mybir.dt.float8_e5m2_x4
E2M1 = mybir.dt.float4_e2m1fn_x4
ALU = mybir.AluOpType
ACT = mybir.ActivationFunctionType

P = 128
PACK = 4
PER_COL = 16
X_FUSED = (0, 0, 0, 0)
G_FUSED = (0, 128)


def tile_list_directions_offset_listed_spread_kernel(
    tc, xf, ra, ow, gt, rb, fkr, dr_words, dr_scales, bn, offs, offs2, out
):
    nc = tc.nc
    with ExitStack() as ctx:
        keep = ctx.enter_context(tc.tile_pool(name="keep", bufs=1))
        ps_turn = ctx.enter_context(tc.psum_pool(name="ps_turn", bufs=4))
        ps_sum = ctx.enter_context(tc.psum_pool(name="ps_sum", bufs=1))

        def tiles(name, count, shape, dtype):
            return [keep.tile(shape, dtype, name=f"{name}{i}", tag=f"{name}{i}", align_bytes=64) for i in range(count)]

        x_list = keep.tile([P, J // PER_COL], U16, name="x_list")
        g_list = keep.tile([P, J // PER_COL], U16, name="g_list")
        x_rows = tiles("x_rows", PACK, [P, T], F32)
        ow_rows = tiles("ow_rows", PACK, [P, J], F32)
        g_rows = tiles("g_rows", 2, [P, V], F32)
        ra_col = keep.tile([P, PACK], F32, name="ra_col")
        rb_col = keep.tile([P, PACK], F32, name="rb_col")
        fk_col = keep.tile([P, PACK], F32, name="fk_col")
        bn_col = keep.tile([P, 2], F32, name="bn_col")
        dr_codes = keep.tile([P, 2 * R], U8, name="dr_codes", align_bytes=64)
        dr_plane = keep.tile([P, R], U8, name="dr_plane", align_bytes=64)
        ident = keep.tile([P, P], F32, name="ident")

        xf_dealt = xf.rearrange("(m s) t -> s m t", s=PACK)
        ow_dealt = ow.rearrange("(m s) j -> s m j", s=PACK)

        nc.scalar.dma_start(out=rb_col[:], in_=rb.rearrange("o (p t) -> (o p) t", t=PACK))
        nc.scalar.dma_start(out=ra_col[:], in_=ra.rearrange("o (p t) -> (o p) t", t=PACK))
        nc.sync.dma_start(out=g_rows[0][:], in_=gt[0:P, :])
        nc.sync.dma_start(out=g_list[:], in_=offs2)
        nc.sync.dma_start(out=x_list[:], in_=offs)
        for s in range(PACK):
            nc.sync.dma_start(out=x_rows[s][:], in_=xf_dealt[s])
            if s == 1:
                nc.sync.dma_start(out=fk_col[:], in_=fkr.rearrange("o (p t) -> (o p) t", t=PACK))
            if s == PACK - 1:
                nc.sync.dma_start(out=g_rows[1][:], in_=gt[P : 2 * P, :])
            nc.sync.dma_start(out=ow_rows[s][:], in_=ow_dealt[s])
        nc.sync.dma_start(out=bn_col[:], in_=bn.rearrange("o (p t) -> (o p) t", t=2))

        nc.gpsimd.memset(dr_plane[:].bitcast(I32), 0)
        nc.sync.dma_start(out=dr_codes[:].bitcast(I32), in_=dr_words[0].bitcast(I32))
        for q in range(4):
            nc.sync.dma_start(
                out=dr_plane[32 * q : 32 * q + 4, :].bitcast(I32),
                in_=dr_scales[0, 4 * q : 4 * q + 4, :].bitcast(I32),
            )

        ones = keep.tile([P, P], F32, name="ones")
        quadrant = keep.tile([P, 1], F32, name="quadrant")
        count = keep.tile([P, P], F32, name="count", align_bytes=64)
        own = keep.tile([P, 32], F32, name="own", align_bytes=64)
        nc.vector.memset(ones[:], 1.0)
        for q in range(4):
            nc.gpsimd.memset(quadrant[32 * q : 32 * (q + 1), :], 32.0 * q)
        nc.vector.tensor_tensor_scan(
            out=count[:], data0=ones[:], data1=ones[:], initial=quadrant[:], op0=ALU.mult, op1=ALU.add
        )
        nc.vector.transpose(out=own[:], in_=count[:, :32])
        nc.vector.tensor_scalar(
            out=ident[:], in0=count[:], scalar1=quadrant[:], scalar2=own[:, 0:1],
            op0=ALU.subtract, op1=ALU.is_equal,
        )
        unread = keep.tile([P, 1], F32, name="unread")
        nc.scalar.activation(out=unread[:], in_=ones[:, 0:1], func=ACT.Abs_reciprocal_sqrt)

        def spread(name, col, per, bank, copy, tag):
            for t in range(per):
                nc.tensor.transpose(bank[:, t, :], col[:, t : t + 1].to_broadcast([P, P]), ident[:])
            row = keep.tile([P, P * per], F32, name=name, tag=tag)
            copy(out=row[:].rearrange("q (p t) -> q p t", t=per), in_=bank[:].rearrange("q t p -> q p t"))
            return row

        def turn(name, rounded):
            words = rounded[:].bitcast(F32)
            bank = ps_turn.tile([P, 2, P], F32, tag="turn", name=f"{name}_bank")
            for u in range(2):
                nc.tensor.transpose(bank[:, u, :], words[:, u::2], ident[:])
            return bank

        def group_and_quantise(name, banks, fmt, tag):
            grouped = keep.tile([P, len(banks) * J], BF16, name=f"{name}_grouped", tag=tag, align_bytes=64)
            for i, bank in enumerate(banks):
                nc.scalar.copy(
                    out=grouped[:, J * i : J * (i + 1)].bitcast(F32).rearrange("p (c u) -> p c u", u=2),
                    in_=bank[:].rearrange("p u c -> p c u"),
                )
            return quantise(name, grouped, fmt, len(banks))

        def quantise(name, grouped, fmt, count):
            codes = keep.tile([P, count * P], U32, name=f"{name}_codes", align_bytes=64)
            plane = keep.tile([P, count * P], U8, name=f"{name}_plane", align_bytes=64)
            nc.vector.quantize_mx(out=codes[:].bitcast(fmt), scales=plane[:], in_=grouped[:])
            return [(codes[:, P * i : P * (i + 1)].bitcast(fmt), plane[:, P * i : P * (i + 1)]) for i in range(count)]

        def features(s):
            fused = X_FUSED[s]
            cut = fused // PER_COL
            diff = keep.tile([P, J], F32, name=f"diff{s}")
            picked = keep.tile([P, J - fused], F32, name=f"picked{s}")
            nc.scalar.activation(out=picked[:], in_=x_rows[s][:].indirect(x_list[:, cut:]), func=ACT.Copy)
            if fused:
                nc.vector.tensor_tensor(
                    out=diff[:, :fused], in0=x_rows[s][:].indirect(x_list[:, :cut]),
                    in1=ow_rows[s][:, :fused], op=ALU.subtract,
                )
            nc.vector.tensor_tensor(
                out=diff[:, fused:], in0=picked[:], in1=ow_rows[s][:, fused:], op=ALU.subtract
            )
            rounded = keep.tile([P, J], BF16, name=f"u_rounded{s}")
            nc.vector.scalar_tensor_tensor(
                out=rounded[:], in0=diff[:], scalar=fk_col[:, s : s + 1], in1=ra_row[:],
                op0=ALU.mult, op1=ALU.mult,
            )
            return turn(f"u{s}", rounded)

        def gradients(h):
            fused = G_FUSED[h]
            cut = fused // PER_COL
            rounded = keep.tile([P, J], BF16, name=f"g_rounded{h}", tag=f"g_rounded{h}")
            picked = keep.tile([P, J - fused], F32, name=f"g_picked{h}")
            nc.scalar.activation(out=picked[:], in_=g_rows[h][:].indirect(g_list[:, cut:]), func=ACT.Copy)
            if fused:
                weighted = keep.tile([P, fused], F32, name=f"g_weighted{h}")
                nc.vector.tensor_tensor(
                    out=weighted[:], in0=g_rows[h][:].indirect(g_list[:, :cut]),
                    in1=rb_row[:, :fused], op=ALU.mult,
                )
                nc.scalar.copy(out=rounded[:, :fused], in_=weighted[:])
            nc.vector.tensor_tensor(out=rounded[:, fused:], in0=picked[:], in1=rb_row[:, fused:], op=ALU.mult)
            return turn(f"g{h}", rounded)

        def weights_row(name, col):
            bank = ps_turn.tile([P, PACK, P], F32, tag="turn", name=f"{name}_bank")
            return spread(name, col, PACK, bank, nc.vector.tensor_copy, name)

        rb_row = weights_row("rb_row", rb_col)
        ra_row = weights_row("ra_row", ra_col)
        g_bank = [gradients(0)]
        u_bank = [features(0), features(1)]
        g_mx = group_and_quantise("g0", g_bank[:1], E5M2, "x_rows1")
        u_bank.append(features(2))
        u_mx = group_and_quantise("u0", u_bank[:1], E4M3, "x_rows2")
        u_bank.append(features(3))
        g_bank.append(gradients(1))
        u_mx.extend(group_and_quantise("u12", u_bank[1:3], E4M3, "g_rows1"))
        g_mx.extend(group_and_quantise("g1", g_bank[1:], E5M2, "g_rows0"))
        u_mx.extend(group_and_quantise("u3", u_bank[3:], E4M3, "x_rows0"))
        bn_bank = ps_sum.tile([P, 2, P], F32, tag="seen1", name="bn_bank")
        bn_row = spread("bn_row", bn_col, 2, bn_bank, nc.scalar.copy, "g_rounded1")

        moment = [ps_sum.tile([P, PACK, P], F32, name=f"moment{h}") for h in range(2)]
        seen = [ps_sum.tile([P, N], F32, name=f"seen{r}", tag=f"seen{r}") for r in range(2)]
        for h in range(2):
            for s in range(PACK):
                nc.tensor.matmul_mx(
                    out=moment[h][:, s, :], lhsT=u_mx[s][0], lhsT_scale=u_mx[s][1],
                    rhs=g_mx[h][0], rhs_scale=g_mx[h][1], start=True, stop=True,
                )
        for h, copy in enumerate((nc.vector.tensor_copy, nc.scalar.copy)):
            w_grouped = keep.tile([P, PACK * P], BF16, name=f"w_grouped{h}", align_bytes=64)
            copy(
                out=w_grouped[:].rearrange("p (c s) -> p c s", s=PACK),
                in_=moment[h][:].rearrange("p s c -> p c s"),
            )
            w_codes, w_plane = quantise(f"w{h}", w_grouped, E5M2, 1)[0]
            for r in range(2):
                nc.tensor.matmul_mx(
                    out=seen[r][:, P * h : P * (h + 1)],
                    lhsT=dr_codes[:, 2 * P * r : 2 * P * (r + 1)].bitcast(E2M1),
                    lhsT_scale=dr_plane[:, P * r : P * (r + 1)],
                    rhs=w_codes, rhs_scale=w_plane, start=True, stop=True,
                )

        wv = tiles("wv", 2, [P, N], F32)
        total = tiles("total", 2, [P, 1], F32)
        below = tiles("below", 2, [P, N], F32)
        below_sum = tiles("below_sum", 2, [P, 1], F32)
        mean = tiles("mean", 2, [P, 1], F32)
        centred = tiles("centred", 2, [P, N], F32)
        root = tiles("root", 2, [P, 1], F32)
        result = tiles("result", 2, [P, N], F32)
        for r in range(2):
            nc.vector.scalar_tensor_tensor(
                out=wv[r][:], in0=seen[r][:], scalar=1.0, in1=bn_row[:], op0=ALU.mult, op1=ALU.add,
                accum_out=total[r][:],
            )
        for r in range(2):
            nc.scalar.activation(
                out=below[r][:], in_=wv[r][:], func=ACT.Relu, scale=-float(N), bias=total[r][:],
                accum_out=below_sum[r][:],
            )
        for r in range(2):
            nc.vector.tensor_scalar(
                out=mean[r][:], in0=total[r][:], scalar1=1.0 / N, scalar2=None, op0=ALU.mult
            )
        for r in range(2):
            nc.vector.tensor_scalar(
                out=centred[r][:], in0=wv[r][:], scalar1=mean[r][:], scalar2=None, op0=ALU.subtract
            )
        for r in range(2):
            nc.scalar.activation(
                out=root[r][:], in_=below_sum[r][:], func=ACT.Abs_reciprocal_sqrt, scale=2.0 / (N * N), bias=2.0
            )
        for r in range(2):
            nc.vector.tensor_scalar(
                out=result[r][:], in0=centred[r][:], scalar1=root[r][:], scalar2=root[r][:],
                op0=ALU.mult, op1=ALU.mult,
            )
            nc.sync.dma_start(out=out[P * r : P * (r + 1), :], in_=result[r][:])
